import numpy as np
import ml_dtypes


def mxq(x, axis, fmt="e4m3"):
    dtype, down = {"e4m3": (ml_dtypes.float8_e4m3fn, 7), "e5m2": (ml_dtypes.float8_e5m2, 14)}[fmt]
    v = np.moveaxis(np.asarray(x, np.float32).astype(ml_dtypes.bfloat16).astype(np.float64), axis, -1)
    blocks = v.reshape(v.shape[:-1] + (-1, 32))
    amax = np.abs(blocks).max(-1, keepdims=True)
    byte = np.maximum(np.where(amax > 0, np.frexp(amax)[1] - 1 + 127, 0) - down, 1)
    scale = np.exp2(byte - 127.0)
    codes = (blocks / scale).astype(np.float32).astype(dtype).astype(np.float64)
    return np.moveaxis((codes * scale).reshape(v.shape), -1, axis)


WIDE = False


def mx_kscale(k):
    if not WIDE:
        return np.ones(k)
    levels = np.array([10, -10, 5, -5, 0])
    if k % 512:
        return np.exp2(np.random.permutation(np.resize(levels, k // 32))).repeat(32)
    a = np.empty((k // 512, 16))
    for p in range(k // 512):
        a[p, :8] = np.random.permutation(np.resize(levels, 8))
        for g in range(8):
            far = levels[np.abs(levels - a[p, g]) >= 10]
            a[p, g + 8] = far[np.random.randint(len(far))]
    return np.exp2(a.ravel()).repeat(32)


def f64(x):
    return np.asarray(x).astype(np.float64)


def striped(idx):
    return np.tile(idx.reshape(-1, 16).T, (8, 1)).astype(np.uint16)


def unstriped(offs):
    return offs[:16].T.reshape(-1).astype(np.int64)


E2M1 = np.array([0.0, 0.5, 1.0, 1.5, 2.0, 3.0, 4.0, 6.0, -0.0, -0.5, -1.0, -1.5, -2.0, -3.0, -4.0, -6.0])


def pack_weight(w, fmt):
    k, n = w.shape
    w = f64(np.asarray(w, np.float32).astype(ml_dtypes.bfloat16)).reshape(k // 32, 32, n)
    amax = np.abs(w).max(1)
    if fmt == "e4m3":
        byte = np.frexp(amax)[1] - 1 + 127 - 7
    else:
        mant, ex = np.frexp(amax / 6.0)
        byte = np.where(mant > 0.5, ex, ex - 1) + 127
    byte = np.clip(np.where(amax > 0, byte, 1), 1, 254)
    scaled = (w * np.exp2(127.0 - byte)[:, None, :]).reshape(k, n).astype(np.float32)
    by_word = np.ascontiguousarray(scaled.reshape(k // 512, 128, 4, n).transpose(0, 1, 3, 2))
    if fmt == "e4m3":
        words = by_word.astype(ml_dtypes.float8_e4m3fn).view(np.uint8)
    else:
        c = by_word.astype(ml_dtypes.float4_e2m1fn).view(np.uint8) & 0xF
        words = (c[..., 0::2] | (c[..., 1::2] << 4)).reshape(k // 512, 128, 2 * n)
    return np.ascontiguousarray(words), np.ascontiguousarray(byte.astype(np.uint8).reshape(k // 512, 16, n))


def unpack_weight(words, scales, fmt):
    g, _, n = scales.shape
    words = np.ascontiguousarray(words).reshape(g, 128, n, -1)
    if fmt == "e4m3":
        vals = words.view(ml_dtypes.float8_e4m3fn).astype(np.float64)
    else:
        nib = np.empty((g, 128, n, 4), np.uint8)
        nib[..., 0::2] = words & 0xF
        nib[..., 1::2] = words >> 4
        vals = E2M1[nib]
    vals = vals * np.repeat(np.exp2(scales.astype(np.float64) - 127.0), 8, axis=1)[..., None]
    return vals.transpose(0, 1, 3, 2).reshape(g * 512, n)


def planes(y):
    n, m = y.shape
    v = y.astype(np.float32).astype(ml_dtypes.bfloat16).astype(np.float64).reshape(n // 32, 32, m)
    top = np.abs(v).max(1)
    byte = np.clip(np.where(top > 0, np.frexp(top)[1] - 1 + 127 - 7, 1), 1, 254)
    codes = (v * np.exp2(127.0 - byte)[:, None, :]).reshape(n, m).astype(np.float32).astype(ml_dtypes.float8_e4m3fn).view(np.uint8)
    words = codes.reshape(n // 512, 128, 4, m).transpose(0, 1, 3, 2)
    return np.ascontiguousarray(words), np.ascontiguousarray(byte.astype(np.uint8).reshape(n // 512, 16, m))


def gelu(v):
    return 0.5 * v * (1.0 + np.tanh(np.sqrt(2.0 / np.pi) * (v + 0.044715 * v**3)))


K, T, E, C, H, N = 1024, 1024, 4, 128, 512, 512


def by_expert(wq, xq):
    return np.concatenate([wq[e].T @ xq[:, e * C:(e + 1) * C] for e in range(E)], axis=1)


def setup_inputs():
    n = np.random.standard_normal
    s = mx_kscale(K)
    u = mx_kscale(H)
    slot_token = np.concatenate([np.random.permutation(T)[:C] for e in range(E)])
    partner = np.concatenate([np.random.permutation(T) for _ in range(-(-E * C // T))])[:E * C]
    x = pack_weight(n((K, T)) * s[:, None], "e4m3")
    w1 = [pack_weight(m, "e2m1") for m in n((E, K, H)) / np.sqrt(K) / s[None, :, None] * u]
    wp = [pack_weight(m, "e2m1") for m in n((E, K, H)) / np.sqrt(K) / s[None, :, None] * u]
    w2 = [pack_weight(m, "e2m1") for m in n((E, H, N)) / np.sqrt(H) / u[None, :, None]]
    return {
        "x_words": x[0],
        "x_scales": x[1],
        "w1_words": np.stack([m[0] for m in w1]),
        "w1_scales": np.stack([m[1] for m in w1]),
        "wp_words": np.stack([m[0] for m in wp]),
        "wp_scales": np.stack([m[1] for m in wp]),
        "w2_words": np.stack([m[0] for m in w2]),
        "w2_scales": np.stack([m[1] for m in w2]),
        "offs": striped(slot_token),
        "offs2": striped(partner),
    }


def reference(x_words, x_scales, w1_words, w1_scales, wp_words, wp_scales, w2_words, w2_scales, offs, offs2):
    w1 = np.stack([unpack_weight(w1_words[e], w1_scales[e], "e2m1") for e in range(E)])
    wp = np.stack([unpack_weight(wp_words[e], wp_scales[e], "e2m1") for e in range(E)])
    w2 = np.stack([unpack_weight(w2_words[e], w2_scales[e], "e2m1") for e in range(E)])
    idx, idx2 = unstriped(offs), unstriped(offs2)
    x = unpack_weight(x_words, x_scales, "e4m3")
    h = gelu(by_expert(w1, x[:, idx]) + by_expert(wp, x[:, idx2]))
    y = by_expert(w2, mxq(h, 0, "e4m3"))
    out = y
    out_0 = out
    return (out_0,) + planes(out_0)

@@ -1,0 +1,193 @@
+from contextlib import ExitStack
+
+import concourse.mybir as mybir
+from concourse.masks import make_identity
+
+K, T, E, C, H, N = 1024, 1024, 4, 128, 512, 512
+FLOPS = 2 * E * C * (2 * K * H + H * N)
+
+F32 = mybir.dt.float32
+BF16 = mybir.dt.bfloat16
+I32 = mybir.dt.int32
+U32 = mybir.dt.uint32
+U16 = mybir.dt.uint16
+U8 = mybir.dt.uint8
+FP8X4 = mybir.dt.float8_e4m3fn_x4
+FP4X4 = mybir.dt.float4_e2m1fn_x4
+GELU = mybir.ActivationFunctionType.Gelu_apprx_tanh
+
+P = 128
+PASSES = K // 512
+SLOTS = E * C
+LIST_COLS = C // 16
+
+
+def tile_moe_duo_s_gelu_kernel(
+    tc, x_words, x_scales, w1_words, w1_scales, wp_words, wp_scales, w2_words, w2_scales, offs, offs2, out_0, out_1, out_2
+):
+    nc = tc.nc
+    with ExitStack() as ctx:
+        keep = ctx.enter_context(tc.tile_pool(name="keep", bufs=1))
+        work = ctx.enter_context(tc.tile_pool(name="work", bufs=2))
+        psum = ctx.enter_context(tc.psum_pool(name="psum", bufs=2))
+
+        def load_scale_rows(queue, plane, scales):
+            rows = scales.rearrange("e s (q r) w -> r q (e s) w", r=4)
+            for r in range(4):
+                queue.dma_start(
+                    out=plane[r:P:32, :].bitcast(I32).rearrange("q (g w) -> q g w", g=rows.shape[2]),
+                    in_=rows[r].bitcast(I32),
+                )
+
+        def load_weight(name, words, experts):
+            n = len(experts)
+            tile = keep.tile([P, n * words.shape[1], words.shape[3]], U8, name=name, align_bytes=64)
+            src = words[experts[0] : experts[0] + n].rearrange("e s p b -> p (e s) b")
+            nc.sync.dma_start(out=tile[:].bitcast(I32), in_=src.bitcast(I32))
+            return {(e, s): tile[:, j * words.shape[1] + s, :] for j, e in enumerate(experts) for s in range(words.shape[1])}
+
+        xs = keep.tile([P, PASSES * T], U8, name="xs", align_bytes=64)
+        nc.vector.memset(xs[:].bitcast(I32), 0)
+        w1s = keep.tile([P, E * PASSES * H], U8, name="w1s", align_bytes=64)
+        wps = keep.tile([P, E * PASSES * H], U8, name="wps", align_bytes=64)
+        w2s = keep.tile([P, E * N], U8, name="w2s", align_bytes=64)
+        load_scale_rows(nc.gpsimd, wps, wp_scales)
+        ident = keep.tile([P, P], F32, name="ident")
+        make_identity(nc, ident[:])
+
+        lists = [keep.tile([P, E * LIST_COLS], U16, name="list%d" % a) for a in range(2)]
+        xw = keep.tile([P, PASSES * T], I32, name="xw", align_bytes=64)
+
+        nc.sync.dma_start(lists[0][:], offs)
+        load_scale_rows(nc.sync, xs, x_scales.rearrange("(e s) b t -> e s b t", e=1))
+        nc.sync.dma_start(lists[1][:], offs2)
+        nc.sync.dma_start(
+            out=xw[:].rearrange("p (s t) -> p s t", s=PASSES), in_=x_words.rearrange("s p t d -> p s (t d)").bitcast(I32)
+        )
+        w1, wp, w2 = {}, {}, {}
+        load_scale_rows(nc.sync, w1s, w1_scales)
+        w1.update(load_weight("w1a", w1_words, (0, 1)))
+        wp.update(load_weight("wpa", wp_words, (0, 1)))
+        w2.update(load_weight("w2", w2_words, (0, 1, 2, 3)))
+        w1.update(load_weight("w1b", w1_words, (2, 3)))
+        load_scale_rows(nc.sync, w2s, w2_scales)
+        wp.update(load_weight("wpb", wp_words, (2, 3)))
+
+        slot_words = {}
+        planes = {(a, s): keep.tile([P, 2 * C], U8, name="gs%d%d" % (a, s), align_bytes=64) for a in range(2) for s in range(PASSES)}
+
+        def gather_scales(experts):
+            first, n = experts[0], len(experts)
+            for s in range(PASSES):
+                for a in range(2):
+                    found = planes[(a, s)][:, (first % 2) * C : (first % 2 + n) * C]
+                    offsets = lists[a][:, first * LIST_COLS : (first + n) * LIST_COLS]
+                    nc.vector.tensor_copy(found, xs[:, s * T : (s + 1) * T].indirect(offsets))
+
+        def gather_words(e):
+            tile = keep.tile([P, 2 * PASSES * C], U32, name="gw%d" % e, tag="late%d" % (e - 2) if e >= 2 else "early%d" % e, align_bytes=64)
+            for s in range(PASSES):
+                for a in range(2):
+                    found = tile[:, (2 * s + a) * C : (2 * s + a + 1) * C]
+                    window = xw[:, s * T : (s + 1) * T].bitcast(U32)
+                    nc.vector.tensor_copy(found, window.indirect(lists[a][:, e * LIST_COLS : (e + 1) * LIST_COLS]))
+                    slot_words[(a, s, e)] = found
+
+        y_scales = keep.tile([P, SLOTS], U8, name="y_scales", align_bytes=64)
+        out_rows = out_0.rearrange("(p t) j -> p t j", t=4)
+        out_words = out_1[0].rearrange("p j d -> p (j d)").bitcast(I32)
+        stage = {}
+
+        def first_layer(e):
+            pre = psum.tile([P, H], F32, name="pre")
+            steps = [(s, a) for s in range(PASSES) for a in range(2)]
+            for j, (s, a) in enumerate(steps):
+                words, plane = ((w1, w1s), (wp, wps))[a]
+                col = (e * PASSES + s) * H
+                nc.tensor.matmul_mx(
+                    out=pre[:],
+                    lhsT=slot_words[(a, s, e)].bitcast(FP8X4),
+                    lhsT_scale=planes[(a, s)][:, (e % 2) * C : (e % 2 + 1) * C],
+                    rhs=words[(e, s)].bitcast(FP4X4),
+                    rhs_scale=plane[:, col : col + H],
+                    start=(j == 0),
+                    stop=(j == len(steps) - 1),
+                )
+            h_rows = work.tile([P, H], BF16, name="h_rows")
+            nc.scalar.activation(
+                out=h_rows[:].rearrange("s (u p d) -> s u p d", u=2, d=2),
+                in_=pre[:].rearrange("s (p u d) -> s u p d", u=2, d=2),
+                func=GELU,
+            )
+            stage[e] = h_rows
+
+        def turn_hidden(e, copy):
+            pairs = stage[e][:].bitcast(F32)
+            turned = psum.tile([P, 2, C], F32, name="h_turned")
+            for u in range(2):
+                nc.tensor.transpose(turned[:, u, :], pairs[:, u * P : (u + 1) * P], ident[:])
+            h_cols = keep.tile([P, 4 * C], BF16, name="h_cols%d" % e, tag="late%d" % e, align_bytes=64)
+            copy(h_cols[:].bitcast(F32).rearrange("p (s u) -> p s u", u=2), turned[:].rearrange("p u s -> p s u"))
+            h_words = work.tile([P, C], U32, name="h_words", align_bytes=64)
+            h_scales = work.tile([P, C], U8, name="h_scales", align_bytes=64)
+            nc.vector.quantize_mx(out=h_words[:].bitcast(FP8X4), scales=h_scales[:], in_=h_cols[:])
+            stage[e] = (h_words, h_scales)
+
+        def second_layer(e, copy):
+            h_words, h_scales = stage[e]
+            y_sums = psum.tile([P, N], F32, name="y_sums")
+            nc.tensor.matmul_mx(
+                out=y_sums[:],
+                lhsT=h_words[:].bitcast(FP8X4),
+                lhsT_scale=h_scales[:],
+                rhs=w2[(e, 0)].bitcast(FP4X4),
+                rhs_scale=w2s[:, e * N : (e + 1) * N],
+                start=True,
+                stop=True,
+            )
+            y_rows = work.tile([P, 4, P], F32, name="y_rows")
+            copy(y_rows[:], y_sums[:].rearrange("s (p t) -> s t p", t=4))
+            stage[e] = y_rows
+
+        def turn_result(e, copy, rounding):
+            y_rows = stage[e]
+            turned = psum.tile([P, 4, C], F32, name="y_turned")
+            for t in range(4):
+                nc.tensor.transpose(turned[:, t, :], y_rows[:, t, :], ident[:])
+            y_cols = keep.tile([P, 4, C], F32, name="y_cols%d" % e)
+            copy(y_cols[:], turned[:])
+            nc.sync.dma_start(out=out_rows[:, :, e * C : (e + 1) * C], in_=y_cols[:])
+            y_half = work.tile([P, 4 * C], BF16, name="y_half", align_bytes=64)
+            rounding(y_half[:].rearrange("p (s t) -> p s t", t=4), y_cols[:].rearrange("p t s -> p s t"))
+            y_words = keep.tile([P, C], I32, name="y_words%d" % e, align_bytes=64)
+            nc.vector.quantize_mx(out=y_words[:].bitcast(FP8X4), scales=y_scales[:, e * C : (e + 1) * C], in_=y_half[:])
+            nc.sync.dma_start(out=out_words[:, e * C : (e + 1) * C], in_=y_words[:])
+
+        on_scalar, on_vector = nc.scalar.copy, nc.vector.tensor_copy
+        gather_scales((0, 1))
+        gather_words(0)
+        gather_words(1)
+        first_layer(0)
+        first_layer(1)
+        gather_scales((2,))
+        turn_hidden(0, on_scalar)
+        gather_words(2)
+        second_layer(0, on_scalar)
+        gather_scales((3,))
+        turn_hidden(1, on_scalar)
+        gather_words(3)
+        first_layer(2)
+        turn_result(0, on_scalar, on_scalar)
+        second_layer(1, on_scalar)
+        first_layer(3)
+        turn_hidden(2, on_scalar)
+        turn_result(1, on_scalar, on_vector)
+        second_layer(2, on_vector)
+        turn_hidden(3, on_vector)
+        turn_result(2, on_scalar, on_vector)
+        second_layer(3, on_scalar)
+        turn_result(3, on_vector, on_vector)
+
+        scale_rows = out_2[0].rearrange("(q r) j -> r q j", r=4)
+        for r in range(4):
+            nc.scalar.dma_start(out=scale_rows[r].bitcast(I32), in_=y_scales[r:P:32, :].bitcast(I32))

@@ -31,9 +31,9 @@ def tile_moe_duo_s_gelu_kernel(
         work = ctx.enter_context(tc.tile_pool(name="work", bufs=2))
         psum = ctx.enter_context(tc.psum_pool(name="psum", bufs=2))
 
-        def load_scale_rows(queue, plane, scales):
+        def load_scale_rows(queue, plane, scales, which=(0, 1, 2, 3)):
             rows = scales.rearrange("e s (q r) w -> r q (e s) w", r=4)
-            for r in range(4):
+            for r in which:
                 queue.dma_start(
                     out=plane[r:P:32, :].bitcast(I32).rearrange("q (g w) -> q g w", g=rows.shape[2]),
                     in_=rows[r].bitcast(I32),
@@ -47,11 +47,12 @@ def tile_moe_duo_s_gelu_kernel(
             return {(e, s): tile[:, j * words.shape[1] + s, :] for j, e in enumerate(experts) for s in range(words.shape[1])}
 
         xs = keep.tile([P, PASSES * T], U8, name="xs", align_bytes=64)
-        nc.vector.memset(xs[:].bitcast(I32), 0)
+        nc.gpsimd.memset(xs[:, 0:T].bitcast(I32), 0)
+        nc.vector.memset(xs[:, T:].bitcast(I32), 0)
         w1s = keep.tile([P, E * PASSES * H], U8, name="w1s", align_bytes=64)
         wps = keep.tile([P, E * PASSES * H], U8, name="wps", align_bytes=64)
         w2s = keep.tile([P, E * N], U8, name="w2s", align_bytes=64)
-        load_scale_rows(nc.gpsimd, wps, wp_scales)
+        nc.vector.memset(w2s[:].bitcast(I32), 0)
         ident = keep.tile([P, P], F32, name="ident")
         make_identity(nc, ident[:])
 
@@ -61,33 +62,33 @@ def tile_moe_duo_s_gelu_kernel(
         nc.sync.dma_start(lists[0][:], offs)
         load_scale_rows(nc.sync, xs, x_scales.rearrange("(e s) b t -> e s b t", e=1))
         nc.sync.dma_start(lists[1][:], offs2)
+        load_scale_rows(nc.sync, w1s, w1_scales, (0,))
         nc.sync.dma_start(
             out=xw[:].rearrange("p (s t) -> p s t", s=PASSES), in_=x_words.rearrange("s p t d -> p s (t d)").bitcast(I32)
         )
         w1, wp, w2 = {}, {}, {}
-        load_scale_rows(nc.sync, w1s, w1_scales)
-        w1.update(load_weight("w1a", w1_words, (0, 1)))
-        wp.update(load_weight("wpa", wp_words, (0, 1)))
+        load_scale_rows(nc.sync, w1s, w1_scales, (1, 2, 3))
+        load_scale_rows(nc.sync, wps, wp_scales)
+        for e in (0, 1):
+            w1.update(load_weight("w1a%d" % e, w1_words, (e,)))
+            wp.update(load_weight("wpa%d" % e, wp_words, (e,)))
         w2.update(load_weight("w2", w2_words, (0, 1, 2, 3)))
-        w1.update(load_weight("w1b", w1_words, (2, 3)))
         load_scale_rows(nc.sync, w2s, w2_scales)
+        w1.update(load_weight("w1b", w1_words, (2, 3)))
         wp.update(load_weight("wpb", wp_words, (2, 3)))
 
         slot_words = {}
-        planes = {(a, s): keep.tile([P, 2 * C], U8, name="gs%d%d" % (a, s), align_bytes=64) for a in range(2) for s in range(PASSES)}
+        planes = {(a, s): keep.tile([P, SLOTS], U8, name="gs%d%d" % (a, s), align_bytes=64) for a in range(2) for s in range(PASSES)}
 
-        def gather_scales(experts):
-            first, n = experts[0], len(experts)
-            for s in range(PASSES):
-                for a in range(2):
-                    found = planes[(a, s)][:, (first % 2) * C : (first % 2 + n) * C]
-                    offsets = lists[a][:, first * LIST_COLS : (first + n) * LIST_COLS]
-                    nc.vector.tensor_copy(found, xs[:, s * T : (s + 1) * T].indirect(offsets))
+        def gather_scales():
+            for a in range(2):
+                for s in range(PASSES):
+                    nc.vector.tensor_copy(planes[(a, s)][:], xs[:, s * T : (s + 1) * T].indirect(lists[a][:]))
 
         def gather_words(e):
-            tile = keep.tile([P, 2 * PASSES * C], U32, name="gw%d" % e, tag="late%d" % (e - 2) if e >= 2 else "early%d" % e, align_bytes=64)
-            for s in range(PASSES):
-                for a in range(2):
+            tile = keep.tile([P, 2 * PASSES * C], U32, name="gw%d" % e, tag="late0" if e == 3 else "early%d" % e, align_bytes=64)
+            for a in range(2):
+                for s in range(PASSES):
                     found = tile[:, (2 * s + a) * C : (2 * s + a + 1) * C]
                     window = xw[:, s * T : (s + 1) * T].bitcast(U32)
                     nc.vector.tensor_copy(found, window.indirect(lists[a][:, e * LIST_COLS : (e + 1) * LIST_COLS]))
@@ -100,14 +101,14 @@ def tile_moe_duo_s_gelu_kernel(
 
         def first_layer(e):
             pre = psum.tile([P, H], F32, name="pre")
-            steps = [(s, a) for s in range(PASSES) for a in range(2)]
+            steps = [(s, a) for a in range(2) for s in range(PASSES)]
             for j, (s, a) in enumerate(steps):
                 words, plane = ((w1, w1s), (wp, wps))[a]
                 col = (e * PASSES + s) * H
                 nc.tensor.matmul_mx(
                     out=pre[:],
                     lhsT=slot_words[(a, s, e)].bitcast(FP8X4),
-                    lhsT_scale=planes[(a, s)][:, (e % 2) * C : (e % 2 + 1) * C],
+                    lhsT_scale=planes[(a, s)][:, e * C : (e + 1) * C],
                     rhs=words[(e, s)].bitcast(FP4X4),
                     rhs_scale=plane[:, col : col + H],
                     start=(j == 0),
@@ -133,29 +134,42 @@ def tile_moe_duo_s_gelu_kernel(
             nc.vector.quantize_mx(out=h_words[:].bitcast(FP8X4), scales=h_scales[:], in_=h_cols[:])
             stage[e] = (h_words, h_scales)
 
-        def second_layer(e, copy):
-            h_words, h_scales = stage[e]
-            y_sums = psum.tile([P, N], F32, name="y_sums")
-            nc.tensor.matmul_mx(
-                out=y_sums[:],
-                lhsT=h_words[:].bitcast(FP8X4),
-                lhsT_scale=h_scales[:],
-                rhs=w2[(e, 0)].bitcast(FP4X4),
-                rhs_scale=w2s[:, e * N : (e + 1) * N],
-                start=True,
-                stop=True,
-            )
-            y_rows = work.tile([P, 4, P], F32, name="y_rows")
-            copy(y_rows[:], y_sums[:].rearrange("s (p t) -> s t p", t=4))
-            stage[e] = y_rows
+        w2_dealt, w2s_dealt = {}, {}
 
-        def turn_result(e, copy, rounding):
-            y_rows = stage[e]
-            turned = psum.tile([P, 4, C], F32, name="y_turned")
+        def deal_words(e):
+            tile = keep.tile([P, N], U16, name="w2d%d" % e, align_bytes=64)
+            nc.scalar.copy(tile[:].rearrange("p (t m) -> p t m", t=4), w2[(e, 0)].bitcast(U16).rearrange("p (m t) -> p t m", t=4))
+            w2_dealt[e] = tile
+
+        def deal_scales(experts, copy):
+            first, n = experts[0], len(experts)
+            tile = keep.tile([P, n * N], U8, name="w2sd%d" % first, align_bytes=64)
+            copy(
+                tile[:].rearrange("p (e t m) -> p e t m", e=n, t=4),
+                w2s[:, first * N : (first + n) * N].rearrange("p (e m t) -> p e t m", e=n, t=4),
+            )
+            for j, e in enumerate(experts):
+                w2s_dealt[e] = tile[:, j * N : (j + 1) * N]
+
+        def second_layer(e):
+            h_words, h_scales = stage[e]
+            y_sums = psum.tile([P, 4, C], F32, name="y_sums")
             for t in range(4):
-                nc.tensor.transpose(turned[:, t, :], y_rows[:, t, :], ident[:])
+                nc.tensor.matmul_mx(
+                    out=y_sums[:, t, :],
+                    lhsT=w2_dealt[e][:, t * P : (t + 1) * P].bitcast(FP4X4),
+                    lhsT_scale=w2s_dealt[e][:, t * P : (t + 1) * P],
+                    rhs=h_words[:].bitcast(FP8X4),
+                    rhs_scale=h_scales[:],
+                    start=True,
+                    stop=True,
+                )
+            stage[e] = y_sums
+
+        def hand_out(e, copy, rounding):
+            y_sums = stage[e]
             y_cols = keep.tile([P, 4, C], F32, name="y_cols%d" % e)
-            copy(y_cols[:], turned[:])
+            copy(y_cols[:], y_sums[:])
             nc.sync.dma_start(out=out_rows[:, :, e * C : (e + 1) * C], in_=y_cols[:])
             y_half = work.tile([P, 4 * C], BF16, name="y_half", align_bytes=64)
             rounding(y_half[:].rearrange("p (s t) -> p s t", t=4), y_cols[:].rearrange("p t s -> p s t"))
@@ -164,29 +178,32 @@ def tile_moe_duo_s_gelu_kernel(
             nc.sync.dma_start(out=out_words[:, e * C : (e + 1) * C], in_=y_words[:])
 
         on_scalar, on_vector = nc.scalar.copy, nc.vector.tensor_copy
-        gather_scales((0, 1))
+        gather_scales()
         gather_words(0)
         gather_words(1)
+        gather_words(2)
         first_layer(0)
         first_layer(1)
-        gather_scales((2,))
         turn_hidden(0, on_scalar)
-        gather_words(2)
-        second_layer(0, on_scalar)
-        gather_scales((3,))
-        turn_hidden(1, on_scalar)
         gather_words(3)
+        deal_words(0)
+        deal_scales((0,), nc.gpsimd.tensor_copy)
+        deal_scales((1, 2, 3), nc.gpsimd.tensor_copy)
+        turn_hidden(1, on_scalar)
+        second_layer(0)
+        for e in (1, 2, 3):
+            deal_words(e)
         first_layer(2)
-        turn_result(0, on_scalar, on_scalar)
-        second_layer(1, on_scalar)
         first_layer(3)
-        turn_hidden(2, on_scalar)
-        turn_result(1, on_scalar, on_vector)
-        second_layer(2, on_vector)
+        hand_out(0, on_scalar, on_vector)
+        second_layer(1)
+        turn_hidden(2, on_vector)
         turn_hidden(3, on_vector)
-        turn_result(2, on_scalar, on_vector)
-        second_layer(3, on_scalar)
-        turn_result(3, on_vector, on_vector)
+        hand_out(1, on_scalar, on_vector)
+        second_layer(2)
+        second_layer(3)
+        hand_out(2, on_scalar, on_vector)
+        hand_out(3, on_vector, on_vector)
 
         scale_rows = out_2[0].rearrange("(q r) j -> r q j", r=4)
         for r in range(4):

@@ -55,6 +55,7 @@ def tile_moe_duo_s_gelu_kernel(
         nc.vector.memset(w2s[:].bitcast(I32), 0)
         ident = keep.tile([P, P], F32, name="ident")
         make_identity(nc, ident[:])
+        load_scale_rows(nc.gpsimd, w2s, w2_scales)
 
         lists = [keep.tile([P, E * LIST_COLS], U16, name="list%d" % a) for a in range(2)]
         xw = keep.tile([P, PASSES * T], I32, name="xw", align_bytes=64)
@@ -62,39 +63,43 @@ def tile_moe_duo_s_gelu_kernel(
         nc.sync.dma_start(lists[0][:], offs)
         load_scale_rows(nc.sync, xs, x_scales.rearrange("(e s) b t -> e s b t", e=1))
         nc.sync.dma_start(lists[1][:], offs2)
-        load_scale_rows(nc.sync, w1s, w1_scales, (0,))
         nc.sync.dma_start(
             out=xw[:].rearrange("p (s t) -> p s t", s=PASSES), in_=x_words.rearrange("s p t d -> p s (t d)").bitcast(I32)
         )
         w1, wp, w2 = {}, {}, {}
-        load_scale_rows(nc.sync, w1s, w1_scales, (1, 2, 3))
-        load_scale_rows(nc.sync, wps, wp_scales)
-        for e in (0, 1):
-            w1.update(load_weight("w1a%d" % e, w1_words, (e,)))
-            wp.update(load_weight("wpa%d" % e, wp_words, (e,)))
-        w2.update(load_weight("w2", w2_words, (0, 1, 2, 3)))
-        load_scale_rows(nc.sync, w2s, w2_scales)
-        w1.update(load_weight("w1b", w1_words, (2, 3)))
-        wp.update(load_weight("wpb", wp_words, (2, 3)))
+        w1.update(load_weight("w1_0", w1_words, (0,)))
+        load_scale_rows(nc.sync, w1s, w1_scales)
+        load_scale_rows(nc.sync, wps, wp_scales, (0, 1))
+        wp.update(load_weight("wp_0", wp_words, (0,)))
+        load_scale_rows(nc.sync, wps, wp_scales, (2, 3))
+        for e in (1, 2, 3):
+            w1.update(load_weight("w1_%d" % e, w1_words, (e,)))
+            wp.update(load_weight("wp_%d" % e, wp_words, (e,)))
+            if e % 2 == 1:
+                w2.update(load_weight("w2_%d" % e, w2_words, (e - 1, e)))
 
         slot_words = {}
-        planes = {(a, s): keep.tile([P, SLOTS], U8, name="gs%d%d" % (a, s), align_bytes=64) for a in range(2) for s in range(PASSES)}
+        planes = {(a, s): keep.tile([P, 3 * C], U8, name="gs%d%d" % (a, s), align_bytes=64) for a in range(2) for s in range(PASSES)}
 
-        def gather_scales():
+        plane_col = {0: C, 1: 2 * C, 2: 0, 3: C}
+
+        def gather_scales(first):
             for a in range(2):
                 for s in range(PASSES):
-                    nc.vector.tensor_copy(planes[(a, s)][:], xs[:, s * T : (s + 1) * T].indirect(lists[a][:]))
+                    found = planes[(a, s)][:, plane_col[first] : plane_col[first] + 2 * C]
+                    offsets = lists[a][:, first * LIST_COLS : (first + 2) * LIST_COLS]
+                    nc.vector.tensor_copy(found, xs[:, s * T : (s + 1) * T].indirect(offsets))
 
-        def gather_words(e):
-            tile = keep.tile([P, 2 * PASSES * C], U32, name="gw%d" % e, tag="late0" if e == 3 else "early%d" % e, align_bytes=64)
+        def gather_words(e, tag):
+            tile = keep.tile([P, 2, PASSES, C], U32, name="gw%d" % e, tag=tag, align_bytes=64)
             for a in range(2):
                 for s in range(PASSES):
-                    found = tile[:, (2 * s + a) * C : (2 * s + a + 1) * C]
                     window = xw[:, s * T : (s + 1) * T].bitcast(U32)
-                    nc.vector.tensor_copy(found, window.indirect(lists[a][:, e * LIST_COLS : (e + 1) * LIST_COLS]))
-                    slot_words[(a, s, e)] = found
+                    nc.vector.tensor_copy(tile[:, a, s, :], window.indirect(lists[a][:, e * LIST_COLS : (e + 1) * LIST_COLS]))
+                    slot_words[(a, s, e)] = tile[:, a, s, :]
 
         y_scales = keep.tile([P, SLOTS], U8, name="y_scales", align_bytes=64)
+        y_words = keep.tile([P, SLOTS], I32, name="y_words", align_bytes=64)
         out_rows = out_0.rearrange("(p t) j -> p t j", t=4)
         out_words = out_1[0].rearrange("p j d -> p (j d)").bitcast(I32)
         stage = {}
@@ -108,7 +113,7 @@ def tile_moe_duo_s_gelu_kernel(
                 nc.tensor.matmul_mx(
                     out=pre[:],
                     lhsT=slot_words[(a, s, e)].bitcast(FP8X4),
-                    lhsT_scale=planes[(a, s)][:, e * C : (e + 1) * C],
+                    lhsT_scale=planes[(a, s)][:, plane_col[e] : plane_col[e] + C],
                     rhs=words[(e, s)].bitcast(FP4X4),
                     rhs_scale=plane[:, col : col + H],
                     start=(j == 0),
@@ -173,38 +178,40 @@ def tile_moe_duo_s_gelu_kernel(
             nc.sync.dma_start(out=out_rows[:, :, e * C : (e + 1) * C], in_=y_cols[:])
             y_half = work.tile([P, 4 * C], BF16, name="y_half", align_bytes=64)
             rounding(y_half[:].rearrange("p (s t) -> p s t", t=4), y_cols[:].rearrange("p t s -> p s t"))
-            y_words = keep.tile([P, C], I32, name="y_words%d" % e, align_bytes=64)
-            nc.vector.quantize_mx(out=y_words[:].bitcast(FP8X4), scales=y_scales[:, e * C : (e + 1) * C], in_=y_half[:])
-            nc.sync.dma_start(out=out_words[:, e * C : (e + 1) * C], in_=y_words[:])
+            cols = slice(e * C, (e + 1) * C)
+            nc.vector.quantize_mx(out=y_words[:, cols].bitcast(FP8X4), scales=y_scales[:, cols], in_=y_half[:])
+            if e >= E - 2:
+                done = slice(0 if e == E - 2 else e * C, (e + 1) * C)
+                nc.sync.dma_start(out=out_words[:, done], in_=y_words[:, done])
 
         on_scalar, on_vector = nc.scalar.copy, nc.vector.tensor_copy
-        gather_scales()
-        gather_words(0)
-        gather_words(1)
-        gather_words(2)
+        gather_scales(0)
+        gather_words(0, "even")
+        gather_words(1, "odd")
         first_layer(0)
-        first_layer(1)
+        gather_scales(2)
+        gather_words(2, "even")
         turn_hidden(0, on_scalar)
-        gather_words(3)
-        deal_words(0)
-        deal_scales((0,), nc.gpsimd.tensor_copy)
-        deal_scales((1, 2, 3), nc.gpsimd.tensor_copy)
+        first_layer(1)
+        gather_words(3, "late0")
         turn_hidden(1, on_scalar)
-        second_layer(0)
-        for e in (1, 2, 3):
-            deal_words(e)
         first_layer(2)
         first_layer(3)
-        hand_out(0, on_scalar, on_vector)
-        second_layer(1)
+        for e in range(E):
+            deal_words(e)
+        deal_scales((0,), nc.gpsimd.tensor_copy)
+        deal_scales((1, 2, 3), nc.gpsimd.tensor_copy)
+        second_layer(0)
         turn_hidden(2, on_vector)
+        second_layer(1)
         turn_hidden(3, on_vector)
-        hand_out(1, on_scalar, on_vector)
+        hand_out(0, on_scalar, on_vector)
         second_layer(2)
+        hand_out(1, on_scalar, on_vector)
         second_layer(3)
         hand_out(2, on_scalar, on_vector)
         hand_out(3, on_vector, on_vector)
 
         scale_rows = out_2[0].rearrange("(q r) j -> r q j", r=4)
         for r in range(4):
-            nc.scalar.dma_start(out=scale_rows[r].bitcast(I32), in_=y_scales[r:P:32, :].bitcast(I32))
+            (nc.scalar, nc.sync)[r // 3].dma_start(out=scale_rows[r].bitcast(I32), in_=y_scales[r:P:32, :].bitcast(I32))

@@ -28,7 +28,7 @@ def tile_moe_duo_s_gelu_kernel(
     nc = tc.nc
     with ExitStack() as ctx:
         keep = ctx.enter_context(tc.tile_pool(name="keep", bufs=1))
-        work = ctx.enter_context(tc.tile_pool(name="work", bufs=2))
+        work = ctx.enter_context(tc.tile_pool(name="work", bufs=4))
         psum = ctx.enter_context(tc.psum_pool(name="psum", bufs=2))
 
         def load_scale_rows(queue, plane, scales, which=(0, 1, 2, 3)):
@@ -55,7 +55,6 @@ def tile_moe_duo_s_gelu_kernel(
         nc.vector.memset(w2s[:].bitcast(I32), 0)
         ident = keep.tile([P, P], F32, name="ident")
         make_identity(nc, ident[:])
-        load_scale_rows(nc.gpsimd, w2s, w2_scales)
 
         lists = [keep.tile([P, E * LIST_COLS], U16, name="list%d" % a) for a in range(2)]
         xw = keep.tile([P, PASSES * T], I32, name="xw", align_bytes=64)
@@ -67,31 +66,25 @@ def tile_moe_duo_s_gelu_kernel(
             out=xw[:].rearrange("p (s t) -> p s t", s=PASSES), in_=x_words.rearrange("s p t d -> p s (t d)").bitcast(I32)
         )
         w1, wp, w2 = {}, {}, {}
-        w1.update(load_weight("w1_0", w1_words, (0,)))
         load_scale_rows(nc.sync, w1s, w1_scales)
-        load_scale_rows(nc.sync, wps, wp_scales, (0, 1))
-        wp.update(load_weight("wp_0", wp_words, (0,)))
-        load_scale_rows(nc.sync, wps, wp_scales, (2, 3))
-        for e in (1, 2, 3):
+        load_scale_rows(nc.sync, wps, wp_scales)
+        load_scale_rows(nc.sync, w2s, w2_scales)
+        for e in range(E):
             w1.update(load_weight("w1_%d" % e, w1_words, (e,)))
             wp.update(load_weight("wp_%d" % e, wp_words, (e,)))
             if e % 2 == 1:
                 w2.update(load_weight("w2_%d" % e, w2_words, (e - 1, e)))
 
         slot_words = {}
-        planes = {(a, s): keep.tile([P, 3 * C], U8, name="gs%d%d" % (a, s), align_bytes=64) for a in range(2) for s in range(PASSES)}
+        planes = {(a, s): keep.tile([P, SLOTS], U8, name="gs%d%d" % (a, s), align_bytes=64) for a in range(2) for s in range(PASSES)}
 
-        plane_col = {0: C, 1: 2 * C, 2: 0, 3: C}
-
-        def gather_scales(first):
+        def gather_scales():
             for a in range(2):
                 for s in range(PASSES):
-                    found = planes[(a, s)][:, plane_col[first] : plane_col[first] + 2 * C]
-                    offsets = lists[a][:, first * LIST_COLS : (first + 2) * LIST_COLS]
-                    nc.vector.tensor_copy(found, xs[:, s * T : (s + 1) * T].indirect(offsets))
+                    nc.vector.tensor_copy(planes[(a, s)][:], xs[:, s * T : (s + 1) * T].indirect(lists[a][:]))
 
-        def gather_words(e, tag):
-            tile = keep.tile([P, 2, PASSES, C], U32, name="gw%d" % e, tag=tag, align_bytes=64)
+        def gather_words(e):
+            tile = keep.tile([P, 2, PASSES, C], U32, name="gw%d" % e, align_bytes=64)
             for a in range(2):
                 for s in range(PASSES):
                     window = xw[:, s * T : (s + 1) * T].bitcast(U32)
@@ -105,7 +98,7 @@ def tile_moe_duo_s_gelu_kernel(
         stage = {}
 
         def first_layer(e):
-            pre = psum.tile([P, H], F32, name="pre")
+            pre = psum.tile([P, H], F32, name="pre", tag="sums")
             steps = [(s, a) for a in range(2) for s in range(PASSES)]
             for j, (s, a) in enumerate(steps):
                 words, plane = ((w1, w1s), (wp, wps))[a]
@@ -113,7 +106,7 @@ def tile_moe_duo_s_gelu_kernel(
                 nc.tensor.matmul_mx(
                     out=pre[:],
                     lhsT=slot_words[(a, s, e)].bitcast(FP8X4),
-                    lhsT_scale=planes[(a, s)][:, plane_col[e] : plane_col[e] + C],
+                    lhsT_scale=planes[(a, s)][:, e * C : (e + 1) * C],
                     rhs=words[(e, s)].bitcast(FP4X4),
                     rhs_scale=plane[:, col : col + H],
                     start=(j == 0),
@@ -132,7 +125,7 @@ def tile_moe_duo_s_gelu_kernel(
             turned = psum.tile([P, 2, C], F32, name="h_turned")
             for u in range(2):
                 nc.tensor.transpose(turned[:, u, :], pairs[:, u * P : (u + 1) * P], ident[:])
-            h_cols = keep.tile([P, 4 * C], BF16, name="h_cols%d" % e, tag="late%d" % e, align_bytes=64)
+            h_cols = keep.tile([P, 4 * C], BF16, name="h_cols%d" % e, align_bytes=64)
             copy(h_cols[:].bitcast(F32).rearrange("p (s u) -> p s u", u=2), turned[:].rearrange("p u s -> p s u"))
             h_words = work.tile([P, C], U32, name="h_words", align_bytes=64)
             h_scales = work.tile([P, C], U8, name="h_scales", align_bytes=64)
@@ -158,7 +151,7 @@ def tile_moe_duo_s_gelu_kernel(
 
         def second_layer(e):
             h_words, h_scales = stage[e]
-            y_sums = psum.tile([P, 4, C], F32, name="y_sums")
+            y_sums = psum.tile([P, 4, C], F32, name="y_sums", tag="sums")
             for t in range(4):
                 nc.tensor.matmul_mx(
                     out=y_sums[:, t, :],
@@ -177,7 +170,9 @@ def tile_moe_duo_s_gelu_kernel(
             copy(y_cols[:], y_sums[:])
             nc.sync.dma_start(out=out_rows[:, :, e * C : (e + 1) * C], in_=y_cols[:])
             y_half = work.tile([P, 4 * C], BF16, name="y_half", align_bytes=64)
-            rounding(y_half[:].rearrange("p (s t) -> p s t", t=4), y_cols[:].rearrange("p t s -> p s t"))
+            rounding(
+                y_half[:].rearrange("p (c i t) -> p c t i", i=4, t=4), y_cols[:].rearrange("p t (c i) -> p c t i", i=4)
+            )
             cols = slice(e * C, (e + 1) * C)
             nc.vector.quantize_mx(out=y_words[:, cols].bitcast(FP8X4), scales=y_scales[:, cols], in_=y_half[:])
             if e >= E - 2:
@@ -185,26 +180,21 @@ def tile_moe_duo_s_gelu_kernel(
                 nc.sync.dma_start(out=out_words[:, done], in_=y_words[:, done])
 
         on_scalar, on_vector = nc.scalar.copy, nc.vector.tensor_copy
-        gather_scales(0)
-        gather_words(0, "even")
-        gather_words(1, "odd")
+        gather_scales()
+        for e in range(E):
+            gather_words(e)
         first_layer(0)
-        gather_scales(2)
-        gather_words(2, "even")
-        turn_hidden(0, on_scalar)
-        first_layer(1)
-        gather_words(3, "late0")
-        turn_hidden(1, on_scalar)
-        first_layer(2)
-        first_layer(3)
+        for e in range(1, E):
+            first_layer(e)
+            if e < E - 1:
+                turn_hidden(e - 1, on_scalar)
         for e in range(E):
             deal_words(e)
-        deal_scales((0,), nc.gpsimd.tensor_copy)
-        deal_scales((1, 2, 3), nc.gpsimd.tensor_copy)
-        second_layer(0)
+        deal_scales((0, 1, 2, 3), on_vector)
         turn_hidden(2, on_vector)
-        second_layer(1)
         turn_hidden(3, on_vector)
+        second_layer(0)
+        second_layer(1)
         hand_out(0, on_scalar, on_vector)
         second_layer(2)
         hand_out(1, on_scalar, on_vector)

@@ -61,35 +61,36 @@ def tile_moe_duo_s_gelu_kernel(
 
         nc.sync.dma_start(lists[0][:], offs)
         load_scale_rows(nc.sync, xs, x_scales.rearrange("(e s) b t -> e s b t", e=1))
-        nc.sync.dma_start(lists[1][:], offs2)
         nc.sync.dma_start(
             out=xw[:].rearrange("p (s t) -> p s t", s=PASSES), in_=x_words.rearrange("s p t d -> p s (t d)").bitcast(I32)
         )
+        nc.sync.dma_start(lists[1][:], offs2)
         w1, wp, w2 = {}, {}, {}
+        w1.update(load_weight("w1_0", w1_words, (0, 1)))
         load_scale_rows(nc.sync, w1s, w1_scales)
         load_scale_rows(nc.sync, wps, wp_scales)
-        load_scale_rows(nc.sync, w2s, w2_scales)
         for e in range(E):
-            w1.update(load_weight("w1_%d" % e, w1_words, (e,)))
+            if e >= 2:
+                w1.update(load_weight("w1_%d" % e, w1_words, (e,)))
             wp.update(load_weight("wp_%d" % e, wp_words, (e,)))
+            if e == 1:
+                load_scale_rows(nc.sync, w2s, w2_scales)
             if e % 2 == 1:
                 w2.update(load_weight("w2_%d" % e, w2_words, (e - 1, e)))
 
         slot_words = {}
         planes = {(a, s): keep.tile([P, SLOTS], U8, name="gs%d%d" % (a, s), align_bytes=64) for a in range(2) for s in range(PASSES)}
 
-        def gather_scales():
-            for a in range(2):
-                for s in range(PASSES):
-                    nc.vector.tensor_copy(planes[(a, s)][:], xs[:, s * T : (s + 1) * T].indirect(lists[a][:]))
+        def gather_scales(a):
+            for s in range(PASSES):
+                nc.vector.tensor_copy(planes[(a, s)][:], xs[:, s * T : (s + 1) * T].indirect(lists[a][:]))
 
-        def gather_words(e):
-            tile = keep.tile([P, 2, PASSES, C], U32, name="gw%d" % e, align_bytes=64)
-            for a in range(2):
-                for s in range(PASSES):
-                    window = xw[:, s * T : (s + 1) * T].bitcast(U32)
-                    nc.vector.tensor_copy(tile[:, a, s, :], window.indirect(lists[a][:, e * LIST_COLS : (e + 1) * LIST_COLS]))
-                    slot_words[(a, s, e)] = tile[:, a, s, :]
+        def gather_words(a, e):
+            tile = keep.tile([P, PASSES, C], U32, name="gw%d%d" % (a, e), tag="gw%d%d" % (a, e if a else e % 2), align_bytes=64)
+            for s in range(PASSES):
+                window = xw[:, s * T : (s + 1) * T].bitcast(U32)
+                nc.vector.tensor_copy(tile[:, s, :], window.indirect(lists[a][:, e * LIST_COLS : (e + 1) * LIST_COLS]))
+                slot_words[(a, s, e)] = tile[:, s, :]
 
         y_scales = keep.tile([P, SLOTS], U8, name="y_scales", align_bytes=64)
         y_words = keep.tile([P, SLOTS], I32, name="y_words", align_bytes=64)
@@ -134,9 +135,9 @@ def tile_moe_duo_s_gelu_kernel(
 
         w2_dealt, w2s_dealt = {}, {}
 
-        def deal_words(e):
+        def deal_words(e, copy):
             tile = keep.tile([P, N], U16, name="w2d%d" % e, align_bytes=64)
-            nc.scalar.copy(tile[:].rearrange("p (t m) -> p t m", t=4), w2[(e, 0)].bitcast(U16).rearrange("p (m t) -> p t m", t=4))
+            copy(tile[:].rearrange("p (t m) -> p t m", t=4), w2[(e, 0)].bitcast(U16).rearrange("p (m t) -> p t m", t=4))
             w2_dealt[e] = tile
 
         def deal_scales(experts, copy):
@@ -180,16 +181,19 @@ def tile_moe_duo_s_gelu_kernel(
                 nc.sync.dma_start(out=out_words[:, done], in_=y_words[:, done])
 
         on_scalar, on_vector = nc.scalar.copy, nc.vector.tensor_copy
-        gather_scales()
+        for a in range(2):
+            gather_scales(a)
+            for e in (0, 1):
+                gather_words(a, e)
         for e in range(E):
-            gather_words(e)
-        first_layer(0)
-        for e in range(1, E):
             first_layer(e)
-            if e < E - 1:
+            if e < 2:
+                for a in range(2):
+                    gather_words(a, e + 2)
+            if e in (1, 2):
                 turn_hidden(e - 1, on_scalar)
         for e in range(E):
-            deal_words(e)
+            deal_words(e, on_scalar if e < 2 else on_vector)
         deal_scales((0, 1, 2, 3), on_vector)
         turn_hidden(2, on_vector)
         turn_hidden(3, on_vector)

from contextlib import ExitStack

import concourse.mybir as mybir
from concourse.masks import make_identity

K, T, E, C, H, N = 1024, 1024, 4, 128, 512, 512
FLOPS = 2 * E * C * (2 * K * H + H * N)

F32 = mybir.dt.float32
BF16 = mybir.dt.bfloat16
I32 = mybir.dt.int32
U32 = mybir.dt.uint32
U16 = mybir.dt.uint16
U8 = mybir.dt.uint8
FP8X4 = mybir.dt.float8_e4m3fn_x4
FP4X4 = mybir.dt.float4_e2m1fn_x4
GELU = mybir.ActivationFunctionType.Gelu_apprx_tanh

P = 128
PASSES = K // 512
SLOTS = E * C
LIST_COLS = C // 16


def tile_moe_duo_s_gelu_kernel(
    tc, x_words, x_scales, w1_words, w1_scales, wp_words, wp_scales, w2_words, w2_scales, offs, offs2, out_0, out_1, out_2
):
    nc = tc.nc
    with ExitStack() as ctx:
        keep = ctx.enter_context(tc.tile_pool(name="keep", bufs=1))
        work = ctx.enter_context(tc.tile_pool(name="work", bufs=4))
        psum = ctx.enter_context(tc.psum_pool(name="psum", bufs=2))

        def load_scale_rows(queue, plane, scales, which=(0, 1, 2, 3)):
            rows = scales.rearrange("e s (q r) w -> r q (e s) w", r=4)
            for r in which:
                queue.dma_start(
                    out=plane[r:P:32, :].bitcast(I32).rearrange("q (g w) -> q g w", g=rows.shape[2]),
                    in_=rows[r].bitcast(I32),
                )

        def load_weight(name, words, experts):
            n = len(experts)
            tile = keep.tile([P, n * words.shape[1], words.shape[3]], U8, name=name, align_bytes=64)
            src = words[experts[0] : experts[0] + n].rearrange("e s p b -> p (e s) b")
            nc.sync.dma_start(out=tile[:].bitcast(I32), in_=src.bitcast(I32))
            return {(e, s): tile[:, j * words.shape[1] + s, :] for j, e in enumerate(experts) for s in range(words.shape[1])}

        xs = keep.tile([P, PASSES * T], U8, name="xs", align_bytes=64)
        nc.gpsimd.memset(xs[:, 0:T].bitcast(I32), 0)
        nc.vector.memset(xs[:, T:].bitcast(I32), 0)
        w1s = keep.tile([P, E * PASSES * H], U8, name="w1s", align_bytes=64)
        wps = keep.tile([P, E * PASSES * H], U8, name="wps", align_bytes=64)
        w2s = keep.tile([P, E * N], U8, name="w2s", align_bytes=64)
        nc.vector.memset(w2s[:].bitcast(I32), 0)
        ident = keep.tile([P, P], F32, name="ident")
        make_identity(nc, ident[:])

        lists = [keep.tile([P, E * LIST_COLS], U16, name="list%d" % a) for a in range(2)]
        xw = keep.tile([P, PASSES * T], I32, name="xw", align_bytes=64)

        nc.sync.dma_start(lists[0][:], offs)
        load_scale_rows(nc.sync, xs, x_scales.rearrange("(e s) b t -> e s b t", e=1))
        nc.sync.dma_start(
            out=xw[:].rearrange("p (s t) -> p s t", s=PASSES), in_=x_words.rearrange("s p t d -> p s (t d)").bitcast(I32)
        )
        nc.sync.dma_start(lists[1][:], offs2)
        w1, wp, w2 = {}, {}, {}
        w1.update(load_weight("w1_0", w1_words, (0, 1)))
        load_scale_rows(nc.sync, w1s, w1_scales)
        load_scale_rows(nc.sync, wps, wp_scales)
        for e in range(E):
            if e >= 2:
                w1.update(load_weight("w1_%d" % e, w1_words, (e,)))
            wp.update(load_weight("wp_%d" % e, wp_words, (e,)))
            if e == 1:
                load_scale_rows(nc.sync, w2s, w2_scales)
            if e % 2 == 1:
                w2.update(load_weight("w2_%d" % e, w2_words, (e - 1, e)))

        slot_words = {}
        planes = {(a, s): keep.tile([P, SLOTS], U8, name="gs%d%d" % (a, s), align_bytes=64) for a in range(2) for s in range(PASSES)}

        def gather_scales(a):
            for s in range(PASSES):
                nc.vector.tensor_copy(planes[(a, s)][:], xs[:, s * T : (s + 1) * T].indirect(lists[a][:]))

        def gather_words(a, e):
            tile = keep.tile([P, PASSES, C], U32, name="gw%d%d" % (a, e), tag="gw%d%d" % (a, e if a else e % 2), align_bytes=64)
            for s in range(PASSES):
                window = xw[:, s * T : (s + 1) * T].bitcast(U32)
                nc.vector.tensor_copy(tile[:, s, :], window.indirect(lists[a][:, e * LIST_COLS : (e + 1) * LIST_COLS]))
                slot_words[(a, s, e)] = tile[:, s, :]

        y_scales = keep.tile([P, SLOTS], U8, name="y_scales", align_bytes=64)
        y_words = keep.tile([P, SLOTS], I32, name="y_words", align_bytes=64)
        out_rows = out_0.rearrange("(p t) j -> p t j", t=4)
        out_words = out_1[0].rearrange("p j d -> p (j d)").bitcast(I32)
        stage = {}

        def first_layer(e):
            pre = psum.tile([P, H], F32, name="pre", tag="sums")
            steps = [(s, a) for a in range(2) for s in range(PASSES)]
            for j, (s, a) in enumerate(steps):
                words, plane = ((w1, w1s), (wp, wps))[a]
                col = (e * PASSES + s) * H
                nc.tensor.matmul_mx(
                    out=pre[:],
                    lhsT=slot_words[(a, s, e)].bitcast(FP8X4),
                    lhsT_scale=planes[(a, s)][:, e * C : (e + 1) * C],
                    rhs=words[(e, s)].bitcast(FP4X4),
                    rhs_scale=plane[:, col : col + H],
                    start=(j == 0),
                    stop=(j == len(steps) - 1),
                )
            h_rows = work.tile([P, H], BF16, name="h_rows")
            nc.scalar.activation(
                out=h_rows[:].rearrange("s (u p d) -> s u p d", u=2, d=2),
                in_=pre[:].rearrange("s (p u d) -> s u p d", u=2, d=2),
                func=GELU,
            )
            stage[e] = h_rows

        def turn_hidden(e, copy):
            pairs = stage[e][:].bitcast(F32)
            turned = psum.tile([P, 2, C], F32, name="h_turned")
            for u in range(2):
                nc.tensor.transpose(turned[:, u, :], pairs[:, u * P : (u + 1) * P], ident[:])
            h_cols = keep.tile([P, 4 * C], BF16, name="h_cols%d" % e, align_bytes=64)
            copy(h_cols[:].bitcast(F32).rearrange("p (s u) -> p s u", u=2), turned[:].rearrange("p u s -> p s u"))
            h_words = work.tile([P, C], U32, name="h_words", align_bytes=64)
            h_scales = work.tile([P, C], U8, name="h_scales", align_bytes=64)
            nc.vector.quantize_mx(out=h_words[:].bitcast(FP8X4), scales=h_scales[:], in_=h_cols[:])
            stage[e] = (h_words, h_scales)

        w2_dealt, w2s_dealt = {}, {}

        def deal_words(e, copy):
            tile = keep.tile([P, N], U16, name="w2d%d" % e, align_bytes=64)
            copy(tile[:].rearrange("p (t m) -> p t m", t=4), w2[(e, 0)].bitcast(U16).rearrange("p (m t) -> p t m", t=4))
            w2_dealt[e] = tile

        def deal_scales(experts, copy):
            first, n = experts[0], len(experts)
            tile = keep.tile([P, n * N], U8, name="w2sd%d" % first, align_bytes=64)
            copy(
                tile[:].rearrange("p (e t m) -> p e t m", e=n, t=4),
                w2s[:, first * N : (first + n) * N].rearrange("p (e m t) -> p e t m", e=n, t=4),
            )
            for j, e in enumerate(experts):
                w2s_dealt[e] = tile[:, j * N : (j + 1) * N]

        def second_layer(e):
            h_words, h_scales = stage[e]
            y_sums = psum.tile([P, 4, C], F32, name="y_sums", tag="sums")
            for t in range(4):
                nc.tensor.matmul_mx(
                    out=y_sums[:, t, :],
                    lhsT=w2_dealt[e][:, t * P : (t + 1) * P].bitcast(FP4X4),
                    lhsT_scale=w2s_dealt[e][:, t * P : (t + 1) * P],
                    rhs=h_words[:].bitcast(FP8X4),
                    rhs_scale=h_scales[:],
                    start=True,
                    stop=True,
                )
            stage[e] = y_sums

        def hand_out(e, copy, rounding):
            y_sums = stage[e]
            y_cols = keep.tile([P, 4, C], F32, name="y_cols%d" % e)
            copy(y_cols[:], y_sums[:])
            nc.sync.dma_start(out=out_rows[:, :, e * C : (e + 1) * C], in_=y_cols[:])
            y_half = work.tile([P, 4 * C], BF16, name="y_half", align_bytes=64)
            rounding(
                y_half[:].rearrange("p (c i t) -> p c t i", i=4, t=4), y_cols[:].rearrange("p t (c i) -> p c t i", i=4)
            )
            cols = slice(e * C, (e + 1) * C)
            nc.vector.quantize_mx(out=y_words[:, cols].bitcast(FP8X4), scales=y_scales[:, cols], in_=y_half[:])
            if e >= E - 2:
                done = slice(0 if e == E - 2 else e * C, (e + 1) * C)
                nc.sync.dma_start(out=out_words[:, done], in_=y_words[:, done])

        on_scalar, on_vector = nc.scalar.copy, nc.vector.tensor_copy
        for a in range(2):
            gather_scales(a)
            for e in (0, 1):
                gather_words(a, e)
        for e in range(E):
            first_layer(e)
            if e < 2:
                for a in range(2):
                    gather_words(a, e + 2)
            if e in (1, 2):
                turn_hidden(e - 1, on_scalar)
        for e in range(E):
            deal_words(e, on_scalar if e < 2 else on_vector)
        deal_scales((0, 1, 2, 3), on_vector)
        turn_hidden(2, on_vector)
        turn_hidden(3, on_vector)
        second_layer(0)
        second_layer(1)
        hand_out(0, on_scalar, on_vector)
        second_layer(2)
        hand_out(1, on_scalar, on_vector)
        second_layer(3)
        hand_out(2, on_scalar, on_vector)
        hand_out(3, on_vector, on_vector)

        scale_rows = out_2[0].rearrange("(q r) j -> r q j", r=4)
        for r in range(4):
            (nc.scalar, nc.sync)[r // 3].dma_start(out=scale_rows[r].bitcast(I32), in_=y_scales[r:P:32, :].bitcast(I32))
